import numpy as np
import ml_dtypes


def mxq(x, axis, fmt="e4m3"):
    dtype, down = {"e4m3": (ml_dtypes.float8_e4m3fn, 7), "e5m2": (ml_dtypes.float8_e5m2, 14)}[fmt]
    v = np.moveaxis(np.asarray(x, np.float32).astype(ml_dtypes.bfloat16).astype(np.float64), axis, -1)
    blocks = v.reshape(v.shape[:-1] + (-1, 32))
    amax = np.abs(blocks).max(-1, keepdims=True)
    byte = np.maximum(np.where(amax > 0, np.frexp(amax)[1] - 1 + 127, 0) - down, 1)
    scale = np.exp2(byte - 127.0)
    codes = (blocks / scale).astype(np.float32).astype(dtype).astype(np.float64)
    return np.moveaxis((codes * scale).reshape(v.shape), -1, axis)


WIDE = False


def mx_kscale(k, group=512):
    if not WIDE:
        return np.ones(k)
    levels = np.array([18, -18])
    if group != 512:
        return np.exp2(np.random.permutation(np.resize(levels, k // group))).repeat(group)
    if k % 512:
        return np.exp2(np.random.permutation(np.resize(levels, k // 32))).repeat(32)
    a = np.empty((k // 512, 16))
    for p in range(k // 512):
        a[p, :8] = np.random.permutation(np.resize(levels, 8))
        for g in range(8):
            far = levels[np.abs(levels - a[p, g]) >= 10]
            a[p, g + 8] = far[np.random.randint(len(far))]
    return np.exp2(a.ravel()).repeat(32)


def f64(x):
    return np.asarray(x).astype(np.float64)


def sigmoid(v):
    return 1.0 / (1.0 + np.exp(-v))


G, D, M, N = 4, 128, 128, 512


def setup_inputs():
    n = np.random.standard_normal
    s_d = mx_kscale(D, 0)
    return {
        "h": (n((G, D, N)) * s_d[:, None]).astype(np.float32),
        "wf": (n((G, D, M)) / np.sqrt(D) / s_d[:, None]).astype(np.float32),
        "wa": (n((G, D, M)) / np.sqrt(D) / s_d[:, None]).astype(np.float32),
        "wb": (n((G, D, M)) / np.sqrt(D) / s_d[:, None]).astype(np.float32),
        "ts": (n((G, M, N))).astype(np.float32),
        "bf": (0.5 * n((G, M, 1))).astype(np.float32),
    }


def reference(h, wf, wa, wb, ts, bf):
    wfq = mxq(f64(wf), 1, "e4m3")
    hq = mxq(f64(h), 1, "e4m3")
    zf = wfq.transpose(0, 2, 1) @ hq
    waq = mxq(f64(wa), 1, "e4m3")
    za = waq.transpose(0, 2, 1) @ hq
    wbq = mxq(f64(wb), 1, "e4m3")
    zb = wbq.transpose(0, 2, 1) @ hq
    s = sigmoid((-(zf + f64(bf))) * f64(ts))
    y = s * np.tanh(za) + (1.0 - s) * np.tanh(zb)
    return y

@@ -1,0 +1,212 @@
+from contextlib import ExitStack
+
+import concourse.mybir as mybir
+
+G, D, M, N = 4, 128, 128, 512
+FLOPS = 3 * 2 * G * D * M * N
+
+F32 = mybir.dt.float32
+BF16 = mybir.dt.bfloat16
+U32 = mybir.dt.uint32
+U8 = mybir.dt.uint8
+FP8X4 = mybir.dt.float8_e4m3fn_x4
+ALU = mybir.AluOpType
+TANH = mybir.ActivationFunctionType.Tanh
+SIGMOID = mybir.ActivationFunctionType.Sigmoid
+
+P = 128
+PACK = 4
+ROWS = D // PACK
+W = 128
+CHUNKS = N // W
+BANK = 512
+
+
+def tile_rows_cell_cfc_kernel(tc, h, wf, wa, wb, ts, bf, out):
+    nc = tc.nc
+    with ExitStack() as ctx:
+        sb = ctx.enter_context(tc.tile_pool(name="sb", bufs=1))
+        ps = ctx.enter_context(tc.psum_pool(name="ps", bufs=1))
+        ctx.enter_context(tc.manual_schedule())
+
+        h_rows = h.rearrange("g (p j) n -> (g p) j n", j=PACK)
+        ts_rows = ts.rearrange("g m n -> m g n")
+        out_rows = out.rearrange("g m n -> m g n")
+        source = {
+            "wf": wf.rearrange("g (p j) m -> (g p) j m", j=PACK),
+            "wa": wa.rearrange("g (p j) m -> (g p) j m", j=PACK),
+            "wb": wb.rearrange("g (p j) m -> (g p) j m", j=PACK),
+        }
+        for c in range(CHUNKS):
+            source["h%d" % c] = h_rows[:, :, c * W : (c + 1) * W]
+
+        raw, grouped, codes, scales = {}, {}, {}, {}
+        for name in source:
+            raw[name] = sb.tile([P, PACK, W], F32, name="raw_" + name, align_bytes=64)
+            grouped[name] = sb.tile([P, W, PACK], BF16, name="grouped_" + name, align_bytes=64)
+            codes[name] = sb.tile([P, W], U32, name="codes_" + name, align_bytes=64)
+            scales[name] = sb.tile([P, W], U8, name="scales_" + name, align_bytes=64)
+
+        def chunk_tiles(name, shape):
+            return [sb.tile(shape, F32, name="%s%d" % (name, c), align_bytes=64) for c in range(CHUNKS)]
+
+        times = chunk_tiles("times", [P, G, W])
+        gate_in = chunk_tiles("gate_in", [P, G, W])
+        gate = chunk_tiles("gate", [P, G, W])
+        cand = chunk_tiles("cand", [P, G, 2, W])
+        diff = chunk_tiles("diff", [P, G, W])
+        mix = chunk_tiles("mix", [P, G, W])
+        res = chunk_tiles("res", [P, G, W])
+        bias = sb.tile([P, G, 8], F32, name="bias")
+        zero_in = sb.tile([P, 8], F32, name="zero_in")
+        zero = sb.tile([P, 8], F32, name="zero")
+        bank_f = [ps.tile([P, BANK], F32, name="bank_f%d" % g) for g in range(G)]
+        bank_ab = [ps.tile([P, BANK], F32, name="bank_ab%d" % g) for g in range(G)]
+
+        def load(name):
+            nc.sync.dma_start(out=raw[name][:], in_=source[name])
+
+        def load_times(c):
+            nc.sync.dma_start(out=times[c][:], in_=ts_rows[:, :, c * W : (c + 1) * W])
+
+        def cast(engine, name, lo=0, hi=W):
+            dst = grouped[name][:, lo:hi, :].rearrange("p (c i) j -> p c j i", i=4)
+            src = raw[name][:, :, lo:hi].rearrange("p j (c i) -> p c j i", i=4)
+            if engine == "vector":
+                nc.vector.tensor_copy(out=dst, in_=src)
+            else:
+                nc.scalar.copy(out=dst, in_=src)
+
+        def quantize(name):
+            nc.vector.quantize_mx(
+                out=codes[name][:].bitcast(FP8X4),
+                scales=scales[name][:],
+                in_=grouped[name][:].rearrange("p n j -> p (n j)"),
+            )
+
+        def product(weight, c):
+            state = "h%d" % c
+            for g in range(G):
+                rows = slice(g * ROWS, (g + 1) * ROWS)
+                if weight == "wf":
+                    dst = bank_f[g][:, c * W : (c + 1) * W]
+                elif weight == "wa":
+                    dst = bank_ab[g][:, 0:W]
+                else:
+                    dst = bank_ab[g][:, W : 2 * W]
+                nc.tensor.matmul_mx(
+                    out=dst,
+                    lhsT=codes[weight][rows, :].bitcast(FP8X4),
+                    lhsT_scale=scales[weight][rows, :],
+                    rhs=codes[state][rows, :].bitcast(FP8X4),
+                    rhs_scale=scales[state][rows, :],
+                    start=True,
+                    stop=True,
+                )
+
+        def candidates(c):
+            for g in range(G):
+                nc.scalar.activation(
+                    out=cand[c][:, g, :, :].rearrange("p a n -> p (a n)"),
+                    in_=bank_ab[g][:, 0 : 2 * W],
+                    func=TANH,
+                )
+
+        def gate_input(c, lo, hi):
+            for g in range(lo, hi):
+                nc.vector.scalar_tensor_tensor(
+                    out=gate_in[c][:, g, :],
+                    in0=bank_f[g][:, c * W : (c + 1) * W],
+                    scalar=bias[:, g, 0:1],
+                    in1=times[c][:, g, :],
+                    op0=ALU.add,
+                    op1=ALU.mult,
+                )
+
+        def gate_tanh(c, lo, hi):
+            nc.scalar.activation(
+                out=gate[c][:, lo:hi, :], in_=gate_in[c][:, lo:hi, :], func=SIGMOID, scale=-1.0
+            )
+
+        def difference(c, lo, hi):
+            nc.vector.tensor_tensor(
+                out=diff[c][:, lo:hi, :], in0=cand[c][:, lo:hi, 0, :], in1=cand[c][:, lo:hi, 1, :], op=ALU.subtract
+            )
+
+        def weigh(c, lo, hi):
+            nc.vector.tensor_tensor(
+                out=mix[c][:, lo:hi, :], in0=gate[c][:, lo:hi, :], in1=diff[c][:, lo:hi, :], op=ALU.mult
+            )
+
+        def finish(c, lo, hi):
+            nc.vector.tensor_tensor(
+                out=res[c][:, lo:hi, :], in0=mix[c][:, lo:hi, :], in1=cand[c][:, lo:hi, 1, :], op=ALU.add
+            )
+            nc.sync.dma_start(out=out_rows[:, lo:hi, c * W : (c + 1) * W], in_=res[c][:, lo:hi, :])
+
+        load("h0")
+        with nc.allow_non_contiguous_dma(reason="one bias value for each partition and head"):
+            nc.scalar.dma_start(out=bias[:, :, 0:1], in_=bf.rearrange("g m o -> m g o"))
+        load("wa")
+        load("wb")
+        load("wf")
+        load("h1")
+        load_times(0)
+        load("h2")
+        load_times(1)
+        load("h3")
+        load_times(2)
+        load_times(3)
+
+        nc.vector.memset(zero_in[:], 0.0)
+        nc.scalar.activation(out=zero[:], in_=zero_in[:], func=SIGMOID)
+
+        cast("vector", "h0")
+        cast("scalar", "wa")
+        quantize("h0")
+        cast("vector", "wb", 0, W // 2)
+        cast("scalar", "wb", W // 2, W)
+        quantize("wa")
+        product("wa", 0)
+        quantize("wb")
+        product("wb", 0)
+        cast("vector", "wf")
+        cast("vector", "h1")
+        quantize("wf")
+        product("wf", 0)
+        quantize("h1")
+        candidates(0)
+        product("wa", 1)
+        product("wb", 1)
+        difference(0, 0, 2)
+        gate_input(0, 0, G)
+        product("wf", 1)
+        difference(0, 2, G)
+        cast("scalar", "h2")
+        gate_tanh(0, 0, G)
+
+        for c in range(CHUNKS - 1):
+            if c + 2 < CHUNKS:
+                quantize("h%d" % (c + 2))
+            gate_input(c + 1, 0, 2)
+            weigh(c, 0, G)
+            gate_input(c + 1, 2, G)
+            candidates(c + 1)
+            if c + 2 < CHUNKS:
+                product("wf", c + 2)
+                product("wa", c + 2)
+                product("wb", c + 2)
+            if c + 3 < CHUNKS:
+                cast("scalar", "h%d" % (c + 3))
+            if c + 2 < CHUNKS:
+                gate_tanh(c + 1, 0, G)
+                finish(c, 0, G)
+                difference(c + 1, 0, G)
+            else:
+                gate_tanh(c + 1, 0, 2)
+                gate_tanh(c + 1, 2, G)
+                finish(c, 0, G)
+        last = CHUNKS - 1
+        for step in (difference, weigh, finish):
+            step(last, 0, 2)
+            step(last, 2, G)

@@ -17,9 +17,9 @@ SIGMOID = mybir.ActivationFunctionType.Sigmoid
 P = 128
 PACK = 4
 ROWS = D // PACK
-W = 128
-CHUNKS = N // W
+MM_N = 128
 BANK = 512
+CHUNKS = [(0, 128), (128, 128), (256, 256)]
 
 
 def tile_rows_cell_cfc_kernel(tc, h, wf, wa, wb, ts, bf, out):
@@ -37,39 +37,46 @@ def tile_rows_cell_cfc_kernel(tc, h, wf, wa, wb, ts, bf, out):
             "wa": wa.rearrange("g (p j) m -> (g p) j m", j=PACK),
             "wb": wb.rearrange("g (p j) m -> (g p) j m", j=PACK),
         }
-        for c in range(CHUNKS):
-            source["h%d" % c] = h_rows[:, :, c * W : (c + 1) * W]
+        for c, (first, width) in enumerate(CHUNKS):
+            source["h%d" % c] = h_rows[:, :, first : first + width]
 
         raw, grouped, codes, scales = {}, {}, {}, {}
         for name in source:
-            raw[name] = sb.tile([P, PACK, W], F32, name="raw_" + name, align_bytes=64)
-            grouped[name] = sb.tile([P, W, PACK], BF16, name="grouped_" + name, align_bytes=64)
-            codes[name] = sb.tile([P, W], U32, name="codes_" + name, align_bytes=64)
-            scales[name] = sb.tile([P, W], U8, name="scales_" + name, align_bytes=64)
+            width = source[name].shape[2]
+            raw[name] = sb.tile([P, PACK, width], F32, name="raw_" + name, align_bytes=64)
+            grouped[name] = sb.tile([P, width, PACK], BF16, name="grouped_" + name, align_bytes=64)
+            codes[name] = sb.tile([P, width], U32, name="codes_" + name, align_bytes=64)
+            scales[name] = sb.tile([P, width], U8, name="scales_" + name, align_bytes=64)
 
-        def chunk_tiles(name, shape):
-            return [sb.tile(shape, F32, name="%s%d" % (name, c), align_bytes=64) for c in range(CHUNKS)]
+        def chunk_tiles(name, *inner):
+            return [
+                sb.tile([P, G, *inner, width], F32, name="%s%d" % (name, c), align_bytes=64)
+                for c, (first, width) in enumerate(CHUNKS)
+            ]
 
-        times = chunk_tiles("times", [P, G, W])
-        gate_in = chunk_tiles("gate_in", [P, G, W])
-        gate = chunk_tiles("gate", [P, G, W])
-        cand = chunk_tiles("cand", [P, G, 2, W])
-        diff = chunk_tiles("diff", [P, G, W])
-        mix = chunk_tiles("mix", [P, G, W])
-        res = chunk_tiles("res", [P, G, W])
-        bias = sb.tile([P, G, 8], F32, name="bias")
-        zero_in = sb.tile([P, 8], F32, name="zero_in")
-        zero = sb.tile([P, 8], F32, name="zero")
+        times = chunk_tiles("times")
+        gate_in = chunk_tiles("gate_in")
+        gate = chunk_tiles("gate")
+        cand = chunk_tiles("cand", 2)
+        diff = chunk_tiles("diff")
+        mix = chunk_tiles("mix")
+        res = chunk_tiles("res")
+        bias_rows = sb.tile([P, G, 32], F32, name="bias_rows", align_bytes=64)
+        bias = sb.tile([P, G, 32], F32, name="bias", align_bytes=64)
+        warm = sb.tile([P, 8], F32, name="warm")
+        warm2 = sb.tile([P, 8], F32, name="warm2")
+        warm_in = sb.tile([P, 8], F32, name="warm_in")
         bank_f = [ps.tile([P, BANK], F32, name="bank_f%d" % g) for g in range(G)]
         bank_ab = [ps.tile([P, BANK], F32, name="bank_ab%d" % g) for g in range(G)]
 
-        def load(name):
-            nc.sync.dma_start(out=raw[name][:], in_=source[name])
+        def load(name, queue=nc.sync):
+            queue.dma_start(out=raw[name][:], in_=source[name])
 
-        def load_times(c):
-            nc.sync.dma_start(out=times[c][:], in_=ts_rows[:, :, c * W : (c + 1) * W])
+        def load_times(c, lo, hi, queue=nc.sync):
+            first, width = CHUNKS[c]
+            queue.dma_start(out=times[c][:, lo:hi, :], in_=ts_rows[:, lo:hi, first : first + width])
 
-        def cast(engine, name, lo=0, hi=W):
+        def cast(engine, name, lo, hi):
             dst = grouped[name][:, lo:hi, :].rearrange("p (c i) j -> p c j i", i=4)
             src = raw[name][:, :, lo:hi].rearrange("p j (c i) -> p c j i", i=4)
             if engine == "vector":
@@ -77,136 +84,157 @@ def tile_rows_cell_cfc_kernel(tc, h, wf, wa, wb, ts, bf, out):
             else:
                 nc.scalar.copy(out=dst, in_=src)
 
-        def quantize(name):
+        def quantize(name, lo, hi):
             nc.vector.quantize_mx(
-                out=codes[name][:].bitcast(FP8X4),
-                scales=scales[name][:],
-                in_=grouped[name][:].rearrange("p n j -> p (n j)"),
+                out=codes[name][:, lo:hi].bitcast(FP8X4),
+                scales=scales[name][:, lo:hi],
+                in_=grouped[name][:, lo:hi, :].rearrange("p n j -> p (n j)"),
             )
 
-        def product(weight, c):
+        def product(weight, c, part=0, lo=0, hi=G):
+            first, width = CHUNKS[c]
             state = "h%d" % c
-            for g in range(G):
+            cols = slice(part * MM_N, (part + 1) * MM_N)
+            for g in range(lo, hi):
                 rows = slice(g * ROWS, (g + 1) * ROWS)
                 if weight == "wf":
-                    dst = bank_f[g][:, c * W : (c + 1) * W]
+                    bank, at = bank_f[g], first
                 elif weight == "wa":
-                    dst = bank_ab[g][:, 0:W]
+                    bank, at = bank_ab[g], 0
                 else:
-                    dst = bank_ab[g][:, W : 2 * W]
+                    bank, at = bank_ab[g], width
+                at += part * MM_N
                 nc.tensor.matmul_mx(
-                    out=dst,
+                    out=bank[:, at : at + MM_N],
                     lhsT=codes[weight][rows, :].bitcast(FP8X4),
                     lhsT_scale=scales[weight][rows, :],
-                    rhs=codes[state][rows, :].bitcast(FP8X4),
-                    rhs_scale=scales[state][rows, :],
+                    rhs=codes[state][rows, cols].bitcast(FP8X4),
+                    rhs_scale=scales[state][rows, cols],
                     start=True,
                     stop=True,
                 )
 
-        def candidates(c):
-            for g in range(G):
+        def candidates(c, lo, hi):
+            first, width = CHUNKS[c]
+            for g in range(lo, hi):
                 nc.scalar.activation(
                     out=cand[c][:, g, :, :].rearrange("p a n -> p (a n)"),
-                    in_=bank_ab[g][:, 0 : 2 * W],
+                    in_=bank_ab[g][:, 0 : 2 * width],
                     func=TANH,
                 )
 
         def gate_input(c, lo, hi):
+            first, width = CHUNKS[c]
             for g in range(lo, hi):
                 nc.vector.scalar_tensor_tensor(
                     out=gate_in[c][:, g, :],
-                    in0=bank_f[g][:, c * W : (c + 1) * W],
+                    in0=bank_f[g][:, first : first + width],
                     scalar=bias[:, g, 0:1],
                     in1=times[c][:, g, :],
                     op0=ALU.add,
                     op1=ALU.mult,
                 )
 
-        def gate_tanh(c, lo, hi):
-            nc.scalar.activation(
-                out=gate[c][:, lo:hi, :], in_=gate_in[c][:, lo:hi, :], func=SIGMOID, scale=-1.0
-            )
+        def gate_sigmoid(c, lo, hi):
+            nc.scalar.activation(out=gate[c][:, lo:hi, :], in_=gate_in[c][:, lo:hi, :], func=SIGMOID, scale=-1.0)
 
-        def difference(c, lo, hi):
-            nc.vector.tensor_tensor(
+        def difference(c, lo, hi, engine=nc.vector):
+            engine.tensor_tensor(
                 out=diff[c][:, lo:hi, :], in0=cand[c][:, lo:hi, 0, :], in1=cand[c][:, lo:hi, 1, :], op=ALU.subtract
             )
 
-        def weigh(c, lo, hi):
-            nc.vector.tensor_tensor(
+        def weigh(c, lo, hi, engine=nc.vector):
+            engine.tensor_tensor(
                 out=mix[c][:, lo:hi, :], in0=gate[c][:, lo:hi, :], in1=diff[c][:, lo:hi, :], op=ALU.mult
             )
 
-        def finish(c, lo, hi):
-            nc.vector.tensor_tensor(
+        def add(c, lo, hi, engine=nc.vector):
+            engine.tensor_tensor(
                 out=res[c][:, lo:hi, :], in0=mix[c][:, lo:hi, :], in1=cand[c][:, lo:hi, 1, :], op=ALU.add
             )
-            nc.sync.dma_start(out=out_rows[:, lo:hi, c * W : (c + 1) * W], in_=res[c][:, lo:hi, :])
+
+        def store(c, lo, hi, queue=nc.sync):
+            first, width = CHUNKS[c]
+            queue.dma_start(out=out_rows[:, lo:hi, first : first + width], in_=res[c][:, lo:hi, :])
+
+        def finish(c, lo, hi, engine=nc.vector):
+            add(c, lo, hi, engine)
+            store(c, lo, hi)
+
+        def load_bias(queue):
+            queue.dma_start(out=bias_rows[0:P:32, :, :], in_=bf.rearrange("g (q j) o -> q g (j o)", j=32))
+
+        def turn_bias():
+            nc.vector.transpose(
+                out=bias[:].rearrange("p g j -> p (g j)"), in_=bias_rows[:].rearrange("p g j -> p (g j)")
+            )
 
         load("h0")
-        with nc.allow_non_contiguous_dma(reason="one bias value for each partition and head"):
-            nc.scalar.dma_start(out=bias[:, :, 0:1], in_=bf.rearrange("g m o -> m g o"))
         load("wa")
         load("wb")
         load("wf")
+        nc.gpsimd.memset(bias_rows[:], 0.0)
+        nc.gpsimd.memset(warm_in[:], 0.0)
+        load_bias(nc.scalar)
+        nc.scalar.activation(out=warm[:], in_=warm_in[:], func=SIGMOID)
         load("h1")
-        load_times(0)
+        load_times(0, 0, G)
         load("h2")
-        load_times(1)
-        load("h3")
-        load_times(2)
-        load_times(3)
+        load_times(1, 0, G)
+        load_times(2, 0, 2)
+        load_times(2, 2, G)
 
-        nc.vector.memset(zero_in[:], 0.0)
-        nc.scalar.activation(out=zero[:], in_=zero_in[:], func=SIGMOID)
-
-        cast("vector", "h0")
-        cast("scalar", "wa")
-        quantize("h0")
-        cast("vector", "wb", 0, W // 2)
-        cast("scalar", "wb", W // 2, W)
-        quantize("wa")
+        cast("vector", "h0", 0, 128)
+        cast("scalar", "wa", 0, 128)
+        quantize("h0", 0, 128)
+        cast("vector", "wb", 0, 64)
+        cast("scalar", "wb", 64, 128)
+        quantize("wa", 0, 128)
         product("wa", 0)
-        quantize("wb")
+        quantize("wb", 0, 128)
         product("wb", 0)
-        cast("vector", "wf")
-        cast("vector", "h1")
-        quantize("wf")
+        cast("vector", "wf", 0, 128)
+        quantize("wf", 0, 128)
         product("wf", 0)
-        quantize("h1")
-        candidates(0)
+        cast("vector", "h1", 0, 128)
+        turn_bias()
+        quantize("h1", 0, 128)
+        candidates(0, 0, G)
         product("wa", 1)
         product("wb", 1)
-        difference(0, 0, 2)
         gate_input(0, 0, G)
         product("wf", 1)
-        difference(0, 2, G)
-        cast("scalar", "h2")
-        gate_tanh(0, 0, G)
-
-        for c in range(CHUNKS - 1):
-            if c + 2 < CHUNKS:
-                quantize("h%d" % (c + 2))
-            gate_input(c + 1, 0, 2)
-            weigh(c, 0, G)
-            gate_input(c + 1, 2, G)
-            candidates(c + 1)
-            if c + 2 < CHUNKS:
-                product("wf", c + 2)
-                product("wa", c + 2)
-                product("wb", c + 2)
-            if c + 3 < CHUNKS:
-                cast("scalar", "h%d" % (c + 3))
-            if c + 2 < CHUNKS:
-                gate_tanh(c + 1, 0, G)
-                finish(c, 0, G)
-                difference(c + 1, 0, G)
-            else:
-                gate_tanh(c + 1, 0, 2)
-                gate_tanh(c + 1, 2, G)
-                finish(c, 0, G)
-        last = CHUNKS - 1
-        for step in (difference, weigh, finish):
-            step(last, 0, 2)
-            step(last, 2, G)
+        gate_sigmoid(0, 0, G)
+        difference(0, 0, G)
+        cast("vector", "h2", 0, 128)
+        cast("scalar", "h2", 128, 256)
+        weigh(0, 0, G)
+        gate_input(1, 0, 2)
+        quantize("h2", 0, 256)
+        gate_input(1, 2, G)
+        candidates(1, 0, G)
+        for lo in (0, 2):
+            for weight in ("wf", "wa", "wb"):
+                product(weight, 2, 0, lo, lo + 2)
+                product(weight, 2, 1, lo, lo + 2)
+        gate_sigmoid(1, 0, G)
+        finish(0, 0, G)
+        difference(1, 0, G)
+        gate_input(2, 0, 2)
+        weigh(1, 0, G)
+        gate_input(2, 2, G)
+        finish(1, 0, G)
+        candidates(2, 0, 2)
+        gate_sigmoid(2, 0, 2)
+        candidates(2, 2, G)
+        gate_sigmoid(2, 2, 3)
+        gate_sigmoid(2, 3, G)
+        difference(2, 0, 2)
+        difference(2, 2, 3)
+        weigh(2, 0, 2)
+        difference(2, 3, G)
+        finish(2, 0, 2)
+        weigh(2, 2, 3)
+        weigh(2, 3, G)
+        finish(2, 2, 3)
+        finish(2, 3, G)

@@ -37,8 +37,8 @@ def tile_rows_cell_cfc_kernel(tc, h, wf, wa, wb, ts, bf, out):
             "wa": wa.rearrange("g (p j) m -> (g p) j m", j=PACK),
             "wb": wb.rearrange("g (p j) m -> (g p) j m", j=PACK),
         }
-        for c, (first, width) in enumerate(CHUNKS):
-            source["h%d" % c] = h_rows[:, :, first : first + width]
+        for k in range(N // MM_N):
+            source["h%d" % k] = h_rows[:, :, k * MM_N : (k + 1) * MM_N]
 
         raw, grouped, codes, scales = {}, {}, {}, {}
         for name in source:
@@ -91,10 +91,11 @@ def tile_rows_cell_cfc_kernel(tc, h, wf, wa, wb, ts, bf, out):
                 in_=grouped[name][:, lo:hi, :].rearrange("p n j -> p (n j)"),
             )
 
-        def product(weight, c, part=0, lo=0, hi=G):
+        def product(weight, k, lo, hi):
+            c = min(k, 2)
+            part = k - c
             first, width = CHUNKS[c]
-            state = "h%d" % c
-            cols = slice(part * MM_N, (part + 1) * MM_N)
+            state = "h%d" % k
             for g in range(lo, hi):
                 rows = slice(g * ROWS, (g + 1) * ROWS)
                 if weight == "wf":
@@ -108,8 +109,8 @@ def tile_rows_cell_cfc_kernel(tc, h, wf, wa, wb, ts, bf, out):
                     out=bank[:, at : at + MM_N],
                     lhsT=codes[weight][rows, :].bitcast(FP8X4),
                     lhsT_scale=scales[weight][rows, :],
-                    rhs=codes[state][rows, cols].bitcast(FP8X4),
-                    rhs_scale=scales[state][rows, cols],
+                    rhs=codes[state][rows, :].bitcast(FP8X4),
+                    rhs_scale=scales[state][rows, :],
                     start=True,
                     stop=True,
                 )
@@ -122,6 +123,12 @@ def tile_rows_cell_cfc_kernel(tc, h, wf, wa, wb, ts, bf, out):
                     in_=bank_ab[g][:, 0 : 2 * width],
                     func=TANH,
                 )
+
+        def candidate(c, g, which):
+            first, width = CHUNKS[c]
+            nc.scalar.activation(
+                out=cand[c][:, g, which, :], in_=bank_ab[g][:, which * width : (which + 1) * width], func=TANH
+            )
 
         def gate_input(c, lo, hi):
             first, width = CHUNKS[c]
@@ -171,70 +178,139 @@ def tile_rows_cell_cfc_kernel(tc, h, wf, wa, wb, ts, bf, out):
 
         load("h0")
         load("wa")
-        load("wb")
         load("wf")
+        load("wb")
         nc.gpsimd.memset(bias_rows[:], 0.0)
         nc.gpsimd.memset(warm_in[:], 0.0)
         load_bias(nc.scalar)
         nc.scalar.activation(out=warm[:], in_=warm_in[:], func=SIGMOID)
         load("h1")
-        load_times(0, 0, G)
+        load_times(0, 0, 4)
         load("h2")
-        load_times(1, 0, G)
+        load("h3")
+        load_times(1, 0, 4)
         load_times(2, 0, 2)
-        load_times(2, 2, G)
-
+        load_times(2, 2, 4)
         cast("vector", "h0", 0, 128)
-        cast("scalar", "wa", 0, 128)
+        cast("vector", "wa", 0, 64)
+        cast("scalar", "wa", 64, 128)
         quantize("h0", 0, 128)
+        quantize("wa", 0, 128)
+        cast("scalar", "wf", 64, 128)
+        cast("vector", "wf", 0, 64)
+        product("wa", 0, 0, 1)
+        product("wa", 0, 1, 2)
+        product("wa", 0, 2, 3)
+        product("wa", 0, 3, 4)
         cast("vector", "wb", 0, 64)
         cast("scalar", "wb", 64, 128)
-        quantize("wa", 0, 128)
-        product("wa", 0)
-        quantize("wb", 0, 128)
-        product("wb", 0)
-        cast("vector", "wf", 0, 128)
         quantize("wf", 0, 128)
-        product("wf", 0)
-        cast("vector", "h1", 0, 128)
+        candidate(0, 0, 0)
+        candidate(0, 1, 0)
+        product("wf", 0, 0, 1)
+        quantize("wb", 0, 128)
+        product("wf", 0, 1, 2)
+        product("wf", 0, 2, 3)
+        product("wf", 0, 3, 4)
+        candidate(0, 2, 0)
         turn_bias()
+        cast("scalar", "h1", 64, 128)
+        cast("vector", "h1", 0, 64)
+        product("wb", 0, 0, 1)
+        product("wb", 0, 1, 2)
+        candidate(0, 3, 0)
+        gate_input(0, 0, 1)
+        product("wb", 0, 2, 3)
+        gate_input(0, 1, 2)
+        candidate(0, 0, 1)
+        gate_input(0, 2, 3)
+        candidate(0, 1, 1)
         quantize("h1", 0, 128)
-        candidates(0, 0, G)
-        product("wa", 1)
-        product("wb", 1)
-        gate_input(0, 0, G)
-        product("wf", 1)
-        gate_sigmoid(0, 0, G)
-        difference(0, 0, G)
+        candidate(0, 2, 1)
+        product("wb", 0, 3, 4)
+        gate_input(0, 3, 4)
+        gate_sigmoid(0, 0, 2)
         cast("vector", "h2", 0, 128)
-        cast("scalar", "h2", 128, 256)
-        weigh(0, 0, G)
-        gate_input(1, 0, 2)
-        quantize("h2", 0, 256)
-        gate_input(1, 2, G)
-        candidates(1, 0, G)
-        for lo in (0, 2):
-            for weight in ("wf", "wa", "wb"):
-                product(weight, 2, 0, lo, lo + 2)
-                product(weight, 2, 1, lo, lo + 2)
-        gate_sigmoid(1, 0, G)
-        finish(0, 0, G)
-        difference(1, 0, G)
-        gate_input(2, 0, 2)
-        weigh(1, 0, G)
-        gate_input(2, 2, G)
-        finish(1, 0, G)
-        candidates(2, 0, 2)
+        product("wf", 1, 0, 1)
+        product("wf", 1, 1, 2)
+        product("wf", 1, 2, 3)
+        candidate(0, 3, 1)
+        gate_sigmoid(0, 2, 4)
+        difference(0, 0, 2, nc.vector)
+        product("wf", 1, 3, 4)
+        product("wa", 1, 0, 1)
+        product("wa", 1, 1, 2)
+        product("wa", 1, 2, 3)
+        quantize("h2", 0, 128)
+        cast("scalar", "h3", 0, 128)
+        product("wa", 1, 3, 4)
+        difference(0, 2, 4, nc.vector)
+        product("wb", 1, 0, 1)
+        product("wb", 1, 1, 2)
+        product("wb", 1, 2, 3)
+        product("wb", 1, 3, 4)
+        weigh(0, 0, 2, nc.vector)
+        candidates(1, 0, 1)
+        gate_input(1, 0, 1)
+        weigh(0, 2, 4, nc.gpsimd)
+        gate_input(1, 1, 2)
+        candidates(1, 1, 2)
+        gate_input(1, 2, 3)
+        gate_input(1, 3, 4)
+        candidates(1, 2, 3)
+        product("wf", 2, 0, 1)
+        difference(1, 0, 1, nc.vector)
+        product("wf", 2, 1, 2)
+        candidates(1, 3, 4)
+        quantize("h3", 0, 128)
+        product("wf", 2, 2, 3)
+        finish(0, 0, 4, nc.vector)
+        product("wf", 2, 3, 4)
+        product("wa", 2, 0, 1)
+        gate_sigmoid(1, 0, 4)
+        product("wa", 2, 1, 2)
+        product("wb", 2, 0, 1)
+        product("wb", 2, 1, 2)
+        difference(1, 1, 4, nc.vector)
+        product("wf", 3, 0, 1)
+        product("wf", 3, 1, 2)
+        product("wa", 3, 0, 1)
+        product("wa", 3, 1, 2)
+        weigh(1, 0, 1, nc.vector)
+        product("wb", 3, 0, 1)
+        product("wb", 3, 1, 2)
+        gate_input(2, 0, 1)
+        product("wf", 3, 2, 3)
+        product("wf", 3, 3, 4)
+        weigh(1, 1, 4, nc.gpsimd)
+        product("wa", 2, 2, 3)
+        gate_input(2, 1, 2)
+        product("wa", 2, 3, 4)
+        candidates(2, 0, 1)
+        product("wb", 2, 2, 3)
+        product("wb", 2, 3, 4)
+        gate_input(2, 2, 3)
+        product("wa", 3, 2, 3)
+        product("wa", 3, 3, 4)
+        gate_input(2, 3, 4)
+        candidates(2, 1, 2)
+        product("wb", 3, 2, 3)
+        product("wb", 3, 3, 4)
+        difference(2, 0, 1, nc.vector)
+        finish(1, 0, 4, nc.vector)
         gate_sigmoid(2, 0, 2)
-        candidates(2, 2, G)
+        difference(2, 1, 2, nc.vector)
+        candidates(2, 2, 3)
+        weigh(2, 0, 1, nc.vector)
+        weigh(2, 1, 2, nc.vector)
+        candidates(2, 3, 4)
+        difference(2, 2, 3, nc.vector)
+        finish(2, 0, 1, nc.vector)
         gate_sigmoid(2, 2, 3)
-        gate_sigmoid(2, 3, G)
-        difference(2, 0, 2)
-        difference(2, 2, 3)
-        weigh(2, 0, 2)
-        difference(2, 3, G)
-        finish(2, 0, 2)
-        weigh(2, 2, 3)
-        weigh(2, 3, G)
-        finish(2, 2, 3)
-        finish(2, 3, G)
+        finish(2, 1, 2, nc.vector)
+        gate_sigmoid(2, 3, 4)
+        difference(2, 3, 4, nc.vector)
+        weigh(2, 2, 3, nc.vector)
+        weigh(2, 3, 4, nc.vector)
+        finish(2, 2, 3, nc.vector)
+        finish(2, 3, 4, nc.vector)

from contextlib import ExitStack

import concourse.mybir as mybir

G, D, M, N = 4, 128, 128, 512
FLOPS = 3 * 2 * G * D * M * N

F32 = mybir.dt.float32
BF16 = mybir.dt.bfloat16
U32 = mybir.dt.uint32
U8 = mybir.dt.uint8
FP8X4 = mybir.dt.float8_e4m3fn_x4
ALU = mybir.AluOpType
TANH = mybir.ActivationFunctionType.Tanh
SIGMOID = mybir.ActivationFunctionType.Sigmoid

P = 128
PACK = 4
ROWS = D // PACK
MM_N = 128
BANK = 512
CHUNKS = [(0, 128), (128, 128), (256, 256)]


def tile_rows_cell_cfc_kernel(tc, h, wf, wa, wb, ts, bf, out):
    nc = tc.nc
    with ExitStack() as ctx:
        sb = ctx.enter_context(tc.tile_pool(name="sb", bufs=1))
        ps = ctx.enter_context(tc.psum_pool(name="ps", bufs=1))
        ctx.enter_context(tc.manual_schedule())

        h_rows = h.rearrange("g (p j) n -> (g p) j n", j=PACK)
        ts_rows = ts.rearrange("g m n -> m g n")
        out_rows = out.rearrange("g m n -> m g n")
        source = {
            "wf": wf.rearrange("g (p j) m -> (g p) j m", j=PACK),
            "wa": wa.rearrange("g (p j) m -> (g p) j m", j=PACK),
            "wb": wb.rearrange("g (p j) m -> (g p) j m", j=PACK),
        }
        for k in range(N // MM_N):
            source["h%d" % k] = h_rows[:, :, k * MM_N : (k + 1) * MM_N]

        raw, grouped, codes, scales = {}, {}, {}, {}
        for name in source:
            width = source[name].shape[2]
            raw[name] = sb.tile([P, PACK, width], F32, name="raw_" + name, align_bytes=64)
            grouped[name] = sb.tile([P, width, PACK], BF16, name="grouped_" + name, align_bytes=64)
            codes[name] = sb.tile([P, width], U32, name="codes_" + name, align_bytes=64)
            scales[name] = sb.tile([P, width], U8, name="scales_" + name, align_bytes=64)

        def chunk_tiles(name, *inner):
            return [
                sb.tile([P, G, *inner, width], F32, name="%s%d" % (name, c), align_bytes=64)
                for c, (first, width) in enumerate(CHUNKS)
            ]

        times = chunk_tiles("times")
        gate_in = chunk_tiles("gate_in")
        gate = chunk_tiles("gate")
        cand = chunk_tiles("cand", 2)
        diff = chunk_tiles("diff")
        mix = chunk_tiles("mix")
        res = chunk_tiles("res")
        bias_rows = sb.tile([P, G, 32], F32, name="bias_rows", align_bytes=64)
        bias = sb.tile([P, G, 32], F32, name="bias", align_bytes=64)
        warm = sb.tile([P, 8], F32, name="warm")
        warm2 = sb.tile([P, 8], F32, name="warm2")
        warm_in = sb.tile([P, 8], F32, name="warm_in")
        bank_f = [ps.tile([P, BANK], F32, name="bank_f%d" % g) for g in range(G)]
        bank_ab = [ps.tile([P, BANK], F32, name="bank_ab%d" % g) for g in range(G)]

        def load(name, queue=nc.sync):
            queue.dma_start(out=raw[name][:], in_=source[name])

        def load_times(c, lo, hi, queue=nc.sync):
            first, width = CHUNKS[c]
            queue.dma_start(out=times[c][:, lo:hi, :], in_=ts_rows[:, lo:hi, first : first + width])

        def cast(engine, name, lo, hi):
            dst = grouped[name][:, lo:hi, :].rearrange("p (c i) j -> p c j i", i=4)
            src = raw[name][:, :, lo:hi].rearrange("p j (c i) -> p c j i", i=4)
            if engine == "vector":
                nc.vector.tensor_copy(out=dst, in_=src)
            else:
                nc.scalar.copy(out=dst, in_=src)

        def quantize(name, lo, hi):
            nc.vector.quantize_mx(
                out=codes[name][:, lo:hi].bitcast(FP8X4),
                scales=scales[name][:, lo:hi],
                in_=grouped[name][:, lo:hi, :].rearrange("p n j -> p (n j)"),
            )

        def product(weight, k, lo, hi):
            c = min(k, 2)
            part = k - c
            first, width = CHUNKS[c]
            state = "h%d" % k
            for g in range(lo, hi):
                rows = slice(g * ROWS, (g + 1) * ROWS)
                if weight == "wf":
                    bank, at = bank_f[g], first
                elif weight == "wa":
                    bank, at = bank_ab[g], 0
                else:
                    bank, at = bank_ab[g], width
                at += part * MM_N
                nc.tensor.matmul_mx(
                    out=bank[:, at : at + MM_N],
                    lhsT=codes[weight][rows, :].bitcast(FP8X4),
                    lhsT_scale=scales[weight][rows, :],
                    rhs=codes[state][rows, :].bitcast(FP8X4),
                    rhs_scale=scales[state][rows, :],
                    start=True,
                    stop=True,
                )

        def candidates(c, lo, hi):
            first, width = CHUNKS[c]
            for g in range(lo, hi):
                nc.scalar.activation(
                    out=cand[c][:, g, :, :].rearrange("p a n -> p (a n)"),
                    in_=bank_ab[g][:, 0 : 2 * width],
                    func=TANH,
                )

        def candidate(c, g, which):
            first, width = CHUNKS[c]
            nc.scalar.activation(
                out=cand[c][:, g, which, :], in_=bank_ab[g][:, which * width : (which + 1) * width], func=TANH
            )

        def gate_input(c, lo, hi):
            first, width = CHUNKS[c]
            for g in range(lo, hi):
                nc.vector.scalar_tensor_tensor(
                    out=gate_in[c][:, g, :],
                    in0=bank_f[g][:, first : first + width],
                    scalar=bias[:, g, 0:1],
                    in1=times[c][:, g, :],
                    op0=ALU.add,
                    op1=ALU.mult,
                )

        def gate_sigmoid(c, lo, hi):
            nc.scalar.activation(out=gate[c][:, lo:hi, :], in_=gate_in[c][:, lo:hi, :], func=SIGMOID, scale=-1.0)

        def difference(c, lo, hi, engine=nc.vector):
            engine.tensor_tensor(
                out=diff[c][:, lo:hi, :], in0=cand[c][:, lo:hi, 0, :], in1=cand[c][:, lo:hi, 1, :], op=ALU.subtract
            )

        def weigh(c, lo, hi, engine=nc.vector):
            engine.tensor_tensor(
                out=mix[c][:, lo:hi, :], in0=gate[c][:, lo:hi, :], in1=diff[c][:, lo:hi, :], op=ALU.mult
            )

        def add(c, lo, hi, engine=nc.vector):
            engine.tensor_tensor(
                out=res[c][:, lo:hi, :], in0=mix[c][:, lo:hi, :], in1=cand[c][:, lo:hi, 1, :], op=ALU.add
            )

        def store(c, lo, hi, queue=nc.sync):
            first, width = CHUNKS[c]
            queue.dma_start(out=out_rows[:, lo:hi, first : first + width], in_=res[c][:, lo:hi, :])

        def finish(c, lo, hi, engine=nc.vector):
            add(c, lo, hi, engine)
            store(c, lo, hi)

        def load_bias(queue):
            queue.dma_start(out=bias_rows[0:P:32, :, :], in_=bf.rearrange("g (q j) o -> q g (j o)", j=32))

        def turn_bias():
            nc.vector.transpose(
                out=bias[:].rearrange("p g j -> p (g j)"), in_=bias_rows[:].rearrange("p g j -> p (g j)")
            )

        load("h0")
        load("wa")
        load("wf")
        load("wb")
        nc.gpsimd.memset(bias_rows[:], 0.0)
        nc.gpsimd.memset(warm_in[:], 0.0)
        load_bias(nc.scalar)
        nc.scalar.activation(out=warm[:], in_=warm_in[:], func=SIGMOID)
        load("h1")
        load_times(0, 0, 4)
        load("h2")
        load("h3")
        load_times(1, 0, 4)
        load_times(2, 0, 2)
        load_times(2, 2, 4)
        cast("vector", "h0", 0, 128)
        cast("vector", "wa", 0, 64)
        cast("scalar", "wa", 64, 128)
        quantize("h0", 0, 128)
        quantize("wa", 0, 128)
        cast("scalar", "wf", 64, 128)
        cast("vector", "wf", 0, 64)
        product("wa", 0, 0, 1)
        product("wa", 0, 1, 2)
        product("wa", 0, 2, 3)
        product("wa", 0, 3, 4)
        cast("vector", "wb", 0, 64)
        cast("scalar", "wb", 64, 128)
        quantize("wf", 0, 128)
        candidate(0, 0, 0)
        candidate(0, 1, 0)
        product("wf", 0, 0, 1)
        quantize("wb", 0, 128)
        product("wf", 0, 1, 2)
        product("wf", 0, 2, 3)
        product("wf", 0, 3, 4)
        candidate(0, 2, 0)
        turn_bias()
        cast("scalar", "h1", 64, 128)
        cast("vector", "h1", 0, 64)
        product("wb", 0, 0, 1)
        product("wb", 0, 1, 2)
        candidate(0, 3, 0)
        gate_input(0, 0, 1)
        product("wb", 0, 2, 3)
        gate_input(0, 1, 2)
        candidate(0, 0, 1)
        gate_input(0, 2, 3)
        candidate(0, 1, 1)
        quantize("h1", 0, 128)
        candidate(0, 2, 1)
        product("wb", 0, 3, 4)
        gate_input(0, 3, 4)
        gate_sigmoid(0, 0, 2)
        cast("vector", "h2", 0, 128)
        product("wf", 1, 0, 1)
        product("wf", 1, 1, 2)
        product("wf", 1, 2, 3)
        candidate(0, 3, 1)
        gate_sigmoid(0, 2, 4)
        difference(0, 0, 2, nc.vector)
        product("wf", 1, 3, 4)
        product("wa", 1, 0, 1)
        product("wa", 1, 1, 2)
        product("wa", 1, 2, 3)
        quantize("h2", 0, 128)
        cast("scalar", "h3", 0, 128)
        product("wa", 1, 3, 4)
        difference(0, 2, 4, nc.vector)
        product("wb", 1, 0, 1)
        product("wb", 1, 1, 2)
        product("wb", 1, 2, 3)
        product("wb", 1, 3, 4)
        weigh(0, 0, 2, nc.vector)
        candidates(1, 0, 1)
        gate_input(1, 0, 1)
        weigh(0, 2, 4, nc.gpsimd)
        gate_input(1, 1, 2)
        candidates(1, 1, 2)
        gate_input(1, 2, 3)
        gate_input(1, 3, 4)
        candidates(1, 2, 3)
        product("wf", 2, 0, 1)
        difference(1, 0, 1, nc.vector)
        product("wf", 2, 1, 2)
        candidates(1, 3, 4)
        quantize("h3", 0, 128)
        product("wf", 2, 2, 3)
        finish(0, 0, 4, nc.vector)
        product("wf", 2, 3, 4)
        product("wa", 2, 0, 1)
        gate_sigmoid(1, 0, 4)
        product("wa", 2, 1, 2)
        product("wb", 2, 0, 1)
        product("wb", 2, 1, 2)
        difference(1, 1, 4, nc.vector)
        product("wf", 3, 0, 1)
        product("wf", 3, 1, 2)
        product("wa", 3, 0, 1)
        product("wa", 3, 1, 2)
        weigh(1, 0, 1, nc.vector)
        product("wb", 3, 0, 1)
        product("wb", 3, 1, 2)
        gate_input(2, 0, 1)
        product("wf", 3, 2, 3)
        product("wf", 3, 3, 4)
        weigh(1, 1, 4, nc.gpsimd)
        product("wa", 2, 2, 3)
        gate_input(2, 1, 2)
        product("wa", 2, 3, 4)
        candidates(2, 0, 1)
        product("wb", 2, 2, 3)
        product("wb", 2, 3, 4)
        gate_input(2, 2, 3)
        product("wa", 3, 2, 3)
        product("wa", 3, 3, 4)
        gate_input(2, 3, 4)
        candidates(2, 1, 2)
        product("wb", 3, 2, 3)
        product("wb", 3, 3, 4)
        difference(2, 0, 1, nc.vector)
        finish(1, 0, 4, nc.vector)
        gate_sigmoid(2, 0, 2)
        difference(2, 1, 2, nc.vector)
        candidates(2, 2, 3)
        weigh(2, 0, 1, nc.vector)
        weigh(2, 1, 2, nc.vector)
        candidates(2, 3, 4)
        difference(2, 2, 3, nc.vector)
        finish(2, 0, 1, nc.vector)
        gate_sigmoid(2, 2, 3)
        finish(2, 1, 2, nc.vector)
        gate_sigmoid(2, 3, 4)
        difference(2, 3, 4, nc.vector)
        weigh(2, 2, 3, nc.vector)
        weigh(2, 3, 4, nc.vector)
        finish(2, 2, 3, nc.vector)
        finish(2, 3, 4, nc.vector)
